import numpy as np, ml_dtypes
CORES = [35,38,43,46]
N = 4
BF = ml_dtypes.bfloat16
def gentries(a):
    return np.ascontiguousarray(a.reshape(8, 16, -1).transpose(0, 2, 1)).reshape(8, -1)
def gtable(e):
    e = np.asarray(e); return np.ascontiguousarray(e.reshape(8, -1, 16).transpose(0, 2, 1)).reshape(128, -1).astype(np.int32)
def f(rng, *shape):
    return (rng.standard_normal(shape, dtype=np.float32) * np.exp2(rng.integers(-2, 3, shape[:-1] + (1,)))).astype(BF)
def wide(rng, *shape):
    v = f(rng, *shape).astype(np.float32); k = shape[:-2] + (1, shape[-1])
    return (v * np.exp2(rng.integers(-6, 7, k)) * (rng.random(k) > 0.0625)).astype(BF)
M, A, L, C, SR, SA = 4096, 1024, 3, 4, 320, 128
def first(l):
    return M + N * SR + (l - 1) * (A + N * SA)
def glists(e):
    return np.stack([gtable(e[r].reshape(8, -1)) for r in range(N)])
def grow(rng, n):
    v = rng.standard_exponential((N, 8, 16, n), dtype=np.float32) * (rng.random((N, 8, 16, n)) < 0.75) * (0.5 + rng.random((N, 8, 1, n)))
    return np.add.accumulate(v, axis=2).reshape(N, 128, n).astype(BF)
def draw_parts(rng):
    e = np.zeros((N, 8, L, 2 * C, A), np.int64); k = (N, 8, 2 * C, A)
    for l in range(1, L + 1):
        e[:, :, l - 1] = rng.integers(0, first(l), k)
        if l > 1: e[:, :, l - 1] = np.where(rng.random(k) < 0.5, rng.integers(first(l - 1), first(l), k), e[:, :, l - 1])
    return e
def draw(rng, e):
    return {"sup": grow(rng, M), "cap": grow(rng, L * A), "stock": (8 * rng.random((N, 128, L * A)) * (rng.random((N, 128, L * A)) < 0.8)).astype(BF), "parts": glists(e),
            "ship": glists(rng.integers(0, M, (N, 8, N * SR))), "hand": glists(rng.integers(0, A, (N, 8, (L - 1) * N * SA)))}
def setup_inputs(rng):
    return draw(rng, draw_parts(rng))
def setup_inputs_ties(rng):
    e = draw_parts(rng); e[:, :, :, 1:C] = np.where(rng.random((N, 8, L, C - 1, A)) < 0.3, e[:, :, :, :1], e[:, :, :, 1:C])
    e[:, :, :, C:] = np.where(rng.random((N, 8, L, C, A)) < 0.2, e[:, :, :, :C], e[:, :, :, C:])
    d = draw(rng, e)
    d["sup"] = np.add.accumulate(rng.integers(0, 2, (N, 8, 16, M)), axis=2).reshape(N, 128, M).astype(np.float32).astype(BF)
    d["cap"] = np.add.accumulate(rng.integers(0, 3, (N, 8, 16, L * A)), axis=2).reshape(N, 128, L * A).astype(np.float32).astype(BF)
    d["stock"] = rng.integers(0, 4, (N, 128, L * A)).astype(np.float32).astype(BF); return d
def setup_inputs_ends(rng):
    e = draw_parts(rng)
    for l in range(1, L + 1):
        b = [0, M - 1, M, M + N * SR - 1]
        for m in range(1, l): b += [first(m), first(m) + A - 1, first(m) + A, first(m + 1) - 1]
        k = (N, 8, 2 * C, A); e[:, :, l - 1] = np.where(rng.random(k) < 0.5, rng.choice(np.array(b), k), e[:, :, l - 1])
        for r in range(N):
            q = (r + 1) % N
            for g in range(8):
                if l == 1: e[r, g, 0, 0, :SR] = M + q * SR + rng.permutation(SR)
                else: e[r, g, l - 1, 0, :SA] = first(l - 1) + A + q * SA + rng.permutation(SA)
    d = draw(rng, e)
    s = rng.integers(0, M, (N, 8, N, SR)); s[..., 0] = 0; s[..., -1] = M - 1; d["ship"] = glists(s)
    h = rng.integers(0, A, (N, 8, L - 1, N, SA)); h[..., 0] = A - 1; h[..., -1] = 0; d["hand"] = glists(h); return d
def setup_inputs_one(rng):
    e = np.zeros((N, 8, L, 2 * C, A), np.int64); a = rng.integers(1, N); k = (8, 2 * C, A)
    for r in range(N):
        q = (r + a) % N; e[r, :, 0] = M + q * SR + rng.integers(0, SR, k)
        for l in range(2, L + 1): e[r, :, l - 1] = first(l - 1) + A + q * SA + rng.integers(0, SA, k)
    d = draw(rng, e); s = rng.integers(0, M, (N, 8, N, SR)); q = rng.integers(0, N); s[q] = s[q][..., :1]; d["ship"] = glists(s); return d
def setup_inputs_late(rng):
    d = setup_inputs(rng); v = d["sup"].astype(np.float32).reshape(N, 8, 16, M); v[:, :, 15] = 64 - v[:, :, 14]; d["sup"] = v.reshape(N, 128, M).astype(BF)
    c = d["cap"].astype(np.float32).reshape(N, 8, 16, L * A); t = rng.integers(0, 14, (N, 8, 1, L * A))
    d["cap"] = np.where(np.arange(16)[:, None] < t - 4, np.float32(0), 8 * c).reshape(N, 128, L * A).astype(BF); return d
def setup_inputs_spread(rng):
    d = setup_inputs(rng)
    for k, n in (("sup", M), ("cap", L * A), ("stock", L * A)): d[k] = (wide(rng, N, 128, n).astype(np.float32) * np.float32(2.0 ** 40)).astype(BF)
    return d
def check_inputs(d):
    bad = []
    try:
        for k in ("sup", "cap", "stock"):
            v = d[k].astype(np.float32)
            if not (np.isfinite(v).all() and (np.abs(v) <= 2.0 ** 60).all()): bad.append(k)
        e = np.stack([gentries(v) for v in d["parts"]]).reshape(N, 8, L, 2 * C * A)
        if any((e[:, :, l - 1] < 0).any() or (e[:, :, l - 1] >= first(l)).any() for l in range(1, L + 1)): bad.append("parts")
        for k, n in (("ship", M), ("hand", A)):
            if (d[k] < 0).any() or (d[k] >= n).any(): bad.append(k)
    except Exception:
        bad.append("shapes")
    return bad
def reference(sup, cap, stock, parts, ship, hand):
    raw = sup.astype(np.float32).reshape(N, 8, 16, M); ca = cap.astype(np.float32).reshape(N, 8, 16, L, A); st = stock.astype(np.float32).reshape(N, 8, 16, L, A)
    e = [gentries(v).reshape(8, L, 1, 2 * C * A) for v in parts]; sh = [gentries(v).reshape(8, 1, N, SR) for v in ship]; ha = [gentries(v).reshape(8, 1, L - 1, N, SA) for v in hand]
    w = np.zeros((N, 8, 16, first(L)), np.float32); now = np.zeros((N, 8, 16, A), np.float32)
    w[..., :M] = raw; h = A // 2
    for r in range(N):
        for q in range(N): w[r, :, :, M + q * SR:M + (q + 1) * SR] = np.take_along_axis(raw[q], sh[q][:, :, r], 2)
    for l in range(1, L + 1):
        for r in range(N):
            v = np.take_along_axis(w[r], e[r][:, l - 1], 2).reshape(8, 16, 2 * C, A)
            i = np.argmin(v[:, 15, :C], axis=1)
            hit = np.arange(C)[:, None] == i[:, None]
            z = np.min(np.where(hit[:, None], v[:, :, C:], v[:, :, :C]), axis=2)
            s = np.zeros_like(z); s[:, 1:, :h] = z[:, :-1, :h]; s[:, 2:, h:] = z[:, :-2, h:]
            now[r] = np.minimum(s, ca[r, :, :, l - 1]) + st[r, :, :, l - 1]
        if l < L:
            b = first(l); w[:, :, :, b:b + A] = now
            for r in range(N):
                for q in range(N): w[r, :, :, b + A + q * SA:b + A + (q + 1) * SA] = np.take_along_axis(now[q], ha[q][:, :, l - 1, r], 2)
    return {"y": now.reshape(N, 128, A)}

@@ -1,0 +1,382 @@
+import numpy as np
+from concourse.bass import DstId, RemoteDMATransfer
+from concourse.mybir import AluOpType, ActivationFunctionType
+
+M, A, L, SR, SA, NR = 4096, 1024, 3, 320, 128, 4
+F32, BF, I32, U16 = "float32", "bfloat16", "int32", "uint16"
+NCH = (3, 5)
+CUM = (0, NCH[0])
+PIECE = 256
+ENG_OFF = 4
+ENG_ON = 4
+NDMA = 32
+
+
+def first(l):
+    return M + NR * SR + (l - 1) * (A + NR * SA)
+
+
+def sb(n, d):
+    return ("sbuf", [128, n], d)
+
+
+SCRATCH = {
+    "Wb": sb(first(1), BF),
+    "W": sb(first(3), F32),
+    "capb": sb(L * A, BF), "stk": sb(L * A, BF), "pt": sb(1536, I32),
+    "shp": sb(80, I32), "shu": sb(80, U16), "hnd": sb(64, I32), "hnu": sb(64, U16),
+    "sb0": sb(3 * SR, BF), "sb1": sb(3 * SA, F32), "sb2": sb(3 * SA, F32),
+    "VV": sb(2048, F32),
+    "PP": sb(2048, F32),
+    "KA": sb(128, F32), "KB": sb(128, F32),
+    "NN": sb(256, F32), "DA": sb(768, F32), "DS": sb(768, F32), "ZA": sb(256, F32), "ZS": sb(512, F32),
+    "OA": sb(64, U16), "OS": sb(128, U16), "KO": sb(768, U16), "II": sb(256, F32), "TT": sb(256, F32),
+    "AL": sb(A, F32), "F1": sb(A, F32), "Z": sb(A, F32), "Zb": sb(A, BF), "Xb": sb(512, BF), "Y": sb(A, F32),
+    "ML": ("sbuf", [128, 2, 8, 32], F32), "MS": sb(256, F32), "ones": sb(128, F32),
+    "Lm": sb(512, F32), "Sm": sb(256, F32), "Sb": sb(256, BF), "Im": sb(128, F32), "Ib": sb(128, BF),
+    "p0": sb(4, I32), "p1": sb(4, I32), "rm": sb(4, F32), "two": sb(64, I32), "pos": sb(64, F32),
+    "J": ("psum", [128, 16, 2, 16], F32),
+    "U0": ("psum", [128, 512], F32), "U1": ("psum", [128, 512], F32), "U2": ("psum", [128, 512], F32),
+    "R": ("psum", [128, 512], F32),
+}
+SEMAPHORES = ["cv", "cs", "ct", "cg"] + ["d%d" % i for i in range(NDMA)] + ["arr0", "arr1", "arr2", "out0", "out1", "out2"]
+
+
+def masks_for(core, dsts, topo):
+    far = [d for d in dsts if topo.chip(d) != topo.chip(core)]
+    near = [d for d in dsts if topo.chip(d) == topo.chip(core)]
+    used, out = set(), {}
+    for part, n in ((far, ENG_OFF), (near, ENG_ON)):
+        seen = set()
+        for i, d in enumerate(part):
+            al = [e for e in topo.engines(core, d) if e not in used]
+            per = len(al) // len(part)
+            mine = al[i * per:(i + 1) * per]
+            out[d] = mine[::max(1, len(mine) // n)][:n]
+            seen |= set(al)
+        used |= seen
+    return {d: (sum(1 << e for e in v), len(v)) for d, v in out.items()}
+
+
+def rank_program(g, core, T, topo):
+    me = T.rank_of(core)
+    if me is None:
+        return
+    cores = list(T.cores)
+    Q = {"v": g.vector, "s": g.scalar, "t": g.tensor, "g": g, "y": g.sync}
+    ops = []
+    V, S, PE, G, SY = "v", "s", "t", "g", "y"
+    Op = AluOpType
+    grid = {n: np.arange(int(np.prod(s[1][1:]))).reshape(s[1][1:]) for n, s in SCRATCH.items()}
+
+    def ap(name, *idx):
+        idx = idx or (slice(None),)
+        return {"ap": T[name][(slice(None),) + tuple(idx)], "buf": name, "cols": grid[name][tuple(idx)].ravel()}
+
+    def c(name, a, b, step=None):
+        return ap(name, slice(a, b, step))
+
+    def op(q, kind, fn, reads, writes, after=(), sem=None, val=None):
+        ops.append({"q": q, "kind": kind, "fn": fn, "r": reads, "w": writes, "after": list(after), "sem": sem, "val": val})
+        return len(ops) - 1
+
+    def ind(win, off):
+        return win["ap"].indirect(off["ap"])
+
+    def copy(q, out, in_):
+        if q == V:
+            return op(V, "c", lambda: g.vector.tensor_copy(out["ap"], in_["ap"]), [in_], [out])
+        return op(S, "c", lambda: g.scalar.activation(out["ap"], in_["ap"], ActivationFunctionType.Copy), [in_], [out])
+
+    def gather(q, out, win, off):
+        if q == V:
+            return op(V, "c", lambda: g.vector.tensor_copy(out["ap"], ind(win, off)), [win, off], [out])
+        return op(S, "c", lambda: g.scalar.activation(out["ap"], ind(win, off), ActivationFunctionType.Copy), [win, off], [out])
+
+    def gmin(out, win, off, in1):
+        return op(V, "c", lambda: g.vector.tensor_tensor(out["ap"], ind(win, off), in1["ap"], Op.min), [win, off, in1], [out])
+
+    def tt(out, in0, in1, alu):
+        return op(V, "c", lambda: g.vector.tensor_tensor(out["ap"], in0["ap"], in1["ap"], alu), [in0, in1], [out])
+
+    def ts(out, in0, scalar, alu):
+        col = [scalar] if isinstance(scalar, dict) else []
+        sc = scalar["ap"] if col else scalar
+        return op(V, "c", lambda: g.vector.tensor_scalar(out["ap"], in0["ap"], sc, None, alu), [in0] + col, [out])
+
+    def scan(out, d0, d1):
+        return op(V, "c", lambda: g.vector.tensor_tensor_scan(out["ap"], d0["ap"], d1["ap"], 0.0, Op.mult, Op.add), [d0, d1], [out])
+
+    def memset(out, v):
+        return op(V, "c", lambda: g.vector.memset(out["ap"], v), [], [out])
+
+    def mm(out, lhsT, rhs, start, stop):
+        return op(PE, "c", lambda: g.tensor.matmul(out["ap"], lhsT["ap"], rhs["ap"], start, stop), [lhsT, rhs], [out])
+
+    def dma(q, out_ap, in_ap, reads, writes, after=()):
+        return op(q, "d", lambda: Q[q].dma_start(out_ap, in_ap), reads, writes, after)
+
+    def load(q, out, src, after=()):
+        return dma(q, out["ap"], src, [], [out], after)
+
+    others = [(me + k) % NR for k in range(1, NR)]
+    others.sort(key=lambda r: topo.chip(cores[r]) == topo.chip(core))
+    mk = masks_for(core, [cores[r] for r in others], topo)
+    n_out = sum(v[1] for v in mk.values())
+    n_in = sum(masks_for(cores[r], [cores[x] for x in range(NR) if x != r], topo)[core][1] for r in others)
+
+    def exchange(k, sbuf, width, land, base, win, offs):
+        cols = width // 16
+        h = cols // 2 - (cols // 2) % 2
+
+        def lst(r, a, b):
+            return c(offs[0], offs[1] + r * cols + a, offs[1] + r * cols + b)
+        gather(V, c(sbuf, 0, width), win, lst(others[0], 0, cols))
+        gather(S, c(sbuf, width, 2 * width), win, lst(others[1], 0, cols))
+        gather(V, c(sbuf, 2 * width, 2 * width + 16 * h), win, lst(others[2], 0, h))
+        gather(S, c(sbuf, 2 * width + 16 * h, 3 * width), win, lst(others[2], h, cols))
+
+        def send():
+            tr = []
+            for i, r in enumerate(others):
+                rid, pid = topo.addr(cores[r])[:2]
+                tr.append(RemoteDMATransfer(dst_ids=[DstId(rid=rid, pnc=pid)], dma_engine_mask=mk[cores[r]][0],
+                                            remote_sem=T.sem["arr%d" % k], src=T[sbuf][:, i * width:(i + 1) * width],
+                                            dst=T[land][:, base + me * width:base + (me + 1) * width]))
+            return g.remote_dma_fused(tr, local_sem=T.sem["out%d" % k])
+        op(G, "r", send, [ap(sbuf)], [], sem="out%d" % k, val=n_out)
+        gather(S, c(land, base + me * width, base + (me + 1) * width), win, lst(me, 0, cols))
+        op(None, "a", None, [], [c(land, base + r * width, base + (r + 1) * width) for r in others], sem="arr%d" % k, val=n_in)
+
+    def steps(lv, buf, order):
+        def lst(i):
+            return c("pt", lv * 512 + order[i] * 64, lv * 512 + order[i] * 64 + 64)
+        for k in range(3):
+            tt(c(buf, lv * 256 + k, lv * 256 + 256, 4), lst(3 - k), lst(2 - k), Op.subtract)
+        copy(V, c(buf, lv * 256 + 3, lv * 256 + 256, 4), lst(0))
+
+    def prepare(lv):
+        pc = lv * 512
+        for e in range(2):
+            for b in range(2):
+                comp = (2, 0)[b] + e
+                copy(V, c("II", e * 128 + b, e * 128 + 128, 2), c("pt", pc + comp * 64, pc + comp * 64 + 64))
+        for u in range(2):
+            for e in range(2):
+                mm(ap("J", slice(0, 8), u), c("Lm", (2 * e + u) * 128, (2 * e + u + 1) * 128), c("II", e * 128, e * 128 + 128), e == 0, e == 1)
+        steps(lv, "DA", (4, 5, 6, 7))
+        steps(lv, "DS", (1, 0, 3, 2))
+        j, t = ap("J", slice(0, 8)), ap("TT")
+        op(V, "c", lambda: g.vector.transpose(t["ap"], j["ap"]), [j], [t])
+        for h in range(2):
+            k0 = lv * 256 + 32 * CUM[h]
+            for ch in range(NCH[h]):
+                bb = CUM[h] + ch
+                copy(V, c("KO", k0 + ch, k0 + 32 * NCH[h], NCH[h]), c("TT", bb * 32, bb * 32 + 32))
+
+    def widen(a, b):
+        copy(S, c("W", a, b), c("Wb", a, b))
+
+    def load_level(lv, after, with_parts):
+        if with_parts:
+            load(SY, c("pt", lv * 512, lv * 512 + 512), T.parts[:, lv * 512:lv * 512 + 512], after)
+        load(SY, c("capb", lv * A, lv * A + A), T.cap[:, lv * A:lv * A + A], after)
+        load(SY, c("stk", lv * A, lv * A + A), T.stock[:, lv * A:lv * A + A], after)
+
+    load(S, ap("shp"), T.ship[:, :])
+    load(SY, c("Wb", 0, M), T.sup[:, :])
+    load(SY, c("pt", 0, 512), T.parts[:, 0:512])
+    load(SY, ap("hnd"), T.hand[:, :])
+    p0, two = ap("p0"), ap("two")
+    op(G, "c", lambda: g.iota(p0["ap"], [[1, 4]], 0, 1), [], [p0])
+    op(G, "c", lambda: g.iota(two["ap"], [[2, 64]], 0, 0), [], [two])
+    for e in range(2):
+        memset(ap("ML", e, slice(None), slice(16 * e, 16 * e + 16)), 1.0)
+        memset(ap("ML", e, slice(None), slice(16 - 16 * e, 32 - 16 * e)), 0.0)
+    memset(ap("MS"), 1.0)
+    memset(ap("ones"), 1.0)
+    memset(c("NN", 0, 256, 4), 0.0)
+    memset(c("MS", 0, 256, 16), 0.0)
+    memset(c("MS", 129, 256, 16), 0.0)
+
+    def select(out, in_, pattern, base):
+        op(G, "c", lambda: g.affine_select(out["ap"], in_["ap"], pattern, Op.is_equal, 0.0, base, 1), [in_], [out])
+    select(ap("Lm"), ap("ML"), [[16, 2], [-16, 2], [-1, 128]], 0)
+    select(ap("Sm"), ap("MS"), [[1, 2], [-1, 128]], 1)
+    select(ap("Im"), ap("ones"), [[-1, 128]], 0)
+    ts(ap("p1"), p0, 15, Op.bitwise_and)
+    for h in range(2):
+        ts(c("rm", h, h + 1), c("p1", 0, 1), float(16 * NCH[h]), Op.mult)
+    for h in range(2):
+        ts(c("pos", 8 * CUM[h], 8 * (CUM[h] + NCH[h])), c("two", 0, 8 * NCH[h]), c("rm", h, h + 1), Op.add)
+    copy(V, ap("shu"), ap("shp"))
+
+    exchange(0, "sb0", SR, "Wb", M, c("Wb", 0, M), ("shu", 0))
+    prepare(0)
+    copy(V, ap("hnu"), ap("hnd"))
+    copy(S, ap("Sb"), ap("Sm"))
+    copy(S, ap("Ib"), ap("Im"))
+    widen(0, 2048)
+
+    for lv in range(L):
+        win = c("Wb" if lv == 0 else "W", 0, first(lv + 1))
+        zn, sn = ("Zb", "Sb") if lv == 0 else ("Z", "Sm")
+        dst, db = ("W", first(lv + 1)) if lv < L - 1 else ("Y", 0)
+        keys = []
+        for h in range(2):
+            n, x0 = NCH[h], 256 * CUM[h]
+            for a in range(0, 256 * n, PIECE):
+                k0 = lv * 256 + 32 * CUM[h] + a // 16
+                vv = c("VV", x0 + a, x0 + a + PIECE)
+                gather(S, vv, win, c("KO", k0, k0 + PIECE // 16))
+                gmin(c("PP", x0 + a, x0 + a + PIECE), win, c("KO", k0 + 16 * n, k0 + 16 * n + PIECE // 16), vv)
+            for kn, src in (("KA", "VV"), ("KB", "PP")):
+                ko = c(kn, 16 * CUM[h], 16 * (CUM[h] + n))
+                keys.append(dma(SY, ko["ap"], T[src][15:128:16, x0:x0 + 256 * n], [c(src, x0, x0 + 256 * n)], [ko]))
+        if lv == 0:
+            load_level(0, [keys[1]], False)
+            widen(2048, 3072)
+        if lv < L - 1:
+            load_level(lv + 1, [keys[3]], True)
+
+        def lists(h):
+            n, m = NCH[h], CUM[h]
+            n0, n1, k0, k1, d0 = 32 * m, 32 * (m + n), 16 * m, 16 * (m + n), lv * 256
+            hi, n3, nn = c("NN", n0 + 2, n1, 4), c("NN", n0 + 3, n1, 4), c("NN", n0, n1)
+            calls = [
+                lambda: tt(c("NN", n0 + 1, n1, 2), c("KA", k0, k1), c("KB", k0, k1), Op.is_gt),
+                lambda: tt(hi, c("KB", k0 + 1, k1, 2), c("KB", k0, k1, 2), Op.is_gt),
+                lambda: tt(n3, n3, hi, Op.max),
+                lambda: scan(c("ZA", n0, n1), nn, c("DA", d0 + n0, d0 + n1)),
+                lambda: copy(V, c("OA", 8 * m, 8 * (m + n)), c("ZA", n0 + 3, n1, 4)),
+                lambda: tt(c("ZS", 2 * n0 + 32 * n + 3, 2 * n1, 4), hi, c("pos", 8 * m, 8 * (m + n)), Op.add),
+                lambda: scan(c("ZS", 2 * n0, 2 * n0 + 32 * n), nn, c("DS", d0 + n0, d0 + n1)),
+                lambda: copy(V, c("OS", k0, k1), c("ZS", 2 * n0 + 3, 2 * n1, 4))]
+            for k in ((0, 1, 2, 3, 4, 5, 6, 7), (1, 0, 5, 2, 3, 6, 4, 7))[h]:
+                calls[k]()
+
+        def alt(a, b):
+            gather(S, c("AL", a, b), win, c("OA", a // 16, b // 16))
+
+        def sib(h, a, b):
+            o = 8 * CUM[h] + a // 16
+            gmin(c("F1", a, b), win, c("OS", o, o + (b - a) // 16), c("AL", a, b))
+
+        def pair(h, un, u0, a, b):
+            n, m = NCH[h], CUM[h]
+            o = 8 * (m + n) + a // 16
+            gmin(c(zn, a, b), c("PP", 256 * m, 256 * (m + n)), c("OS", o, o + (b - a) // 16), c("F1", a, b))
+            for x, y in ((a, min(b, A // 2)), (max(a, A // 2), b)):
+                if x < y:
+                    s0 = 128 * (x >= A // 2)
+                    mm(c(un, x - u0, y - u0), c(sn, s0, s0 + 128), c(zn, x, y), True, True)
+
+        def capped(un, a, b):
+            u = c(un, 0, b - a)
+            tt(u, u, c("capb", lv * A + a, lv * A + b), Op.min)
+
+        def stocked(un, a, b):
+            tt(c(dst, db + a, db + b), c(un, 0, b - a), c("stk", lv * A + a, lv * A + b), Op.add)
+            if lv == L - 1:
+                dma(SY, T.y[:, a:b], T.Y[:, a:b], [c("Y", a, b)], [])
+
+        a1, a2, a3 = 128, 128 * NCH[0], 768
+        lists(0)
+        alt(0, a1)
+        alt(a1, a2)
+        sib(0, 0, a1)
+        pair(0, "U0", 0, 0, a1)
+        sib(0, a1, a2)
+        pair(0, "U0", 0, a1, a2)
+        if lv == 0:
+            widen(3072, 4096)
+        lists(1)
+        alt(a2, a3)
+        alt(a3, A)
+        if lv == 0:
+            tt(c("Xb", 0, a2), c("U0", 0, a2), c("capb", 0, a2), Op.min)
+            mm(c("R", 0, a2), ap("Ib"), c("Xb", 0, a2), True, False)
+            mm(c("R", 0, a2), ap("Ib"), c("stk", 0, a2), False, True)
+            copy(S, c(dst, db, db + a2), c("R", 0, a2))
+            sib(1, a2, a3)
+            sib(1, a3, A)
+            pair(1, "U1", a2, a2, a3)
+        else:
+            capped("U0", 0, a2)
+            sib(1, a2, a3)
+            stocked("U0", 0, a2)
+            pair(1, "U1", a2, a2, a3)
+            sib(1, a3, A)
+        pair(1, "U2", a3, a3, A)
+        capped("U1", a2, a3)
+        if lv == 0:
+            capped("U2", a3, A)
+            stocked("U1", a2, a3)
+        else:
+            stocked("U1", a2, a3)
+            capped("U2", a3, A)
+        stocked("U2", a3, A)
+        if lv < L - 1:
+            exchange(lv + 1, "sb%d" % (lv + 1), SA, "W", db + A, c("W", db, db + A), ("hnu", lv * 32))
+            prepare(lv + 1)
+            if lv == 0:
+                widen(M, first(1))
+
+    csem = {V: "cv", S: "cs", PE: "ct", G: "cg"}
+    count = {k: 0 for k in csem}
+    known = {q: {} for q in Q}
+    hist = {n: [] for n in SCRATCH}
+    final = {}
+    nd = 0
+    for i, o in enumerate(ops):
+        deps = set(o["after"])
+        acc = [(a, False) for a in o["r"]] + [(a, True) for a in o["w"]]
+        for a, wr in acc:
+            psum = SCRATCH[a["buf"]][0] == "psum"
+            mask = np.zeros(grid[a["buf"]].size, bool)
+            mask[a["cols"]] = True
+            for j, m2, w2 in hist[a["buf"]]:
+                if j == i:
+                    continue
+                same = ops[j]["q"] == o["q"]
+                if psum and not same:
+                    deps.add(j)
+                elif psum and o["q"] == PE:
+                    continue
+                elif (wr or w2) and (mask & m2).any():
+                    deps.add(j)
+            hist[a["buf"]].append((i, mask, wr))
+        q = o["q"]
+        if o["kind"] == "a":
+            o["ev"], o["clock"] = (o["sem"], o["val"]), {o["sem"]: o["val"]}
+            final[o["sem"]] = o["val"]
+            continue
+        need = {}
+        for j in deps:
+            s, v = ops[j]["ev"]
+            if v > need.get(s, (0, None))[0]:
+                need[s] = (v, j)
+        for s, (v, j) in sorted(need.items(), key=lambda kv: -kv[1][1]):
+            if known[q].get(s, 0) >= v:
+                continue
+            Q[q].wait_ge(T.sem[s], v)
+            for s2, v2 in ops[j]["clock"].items():
+                known[q][s2] = max(known[q].get(s2, 0), v2)
+        ins = o["fn"]()
+        if o["kind"] == "c":
+            count[q] += 1
+            ev = (csem[q], count[q])
+            ins.then_inc(T.sem[ev[0]], 1)
+        elif o["kind"] == "d":
+            ev = ("d%d" % nd, 16)
+            nd += 1
+            ins.then_inc(T.sem[ev[0]], 16)
+        else:
+            ev = (o["sem"], o["val"])
+        o["ev"] = ev
+        o["clock"] = dict(known[q])
+        o["clock"][ev[0]] = ev[1]
+        final[ev[0]] = ev[1]
+    for s, v in final.items():
+        if max(known[q].get(s, 0) for q in Q) < v:
+            g.sync.wait_ge(T.sem[s], v)

@@ -9,6 +9,7 @@ CUM = (0, NCH[0])
 PIECE = 256
 ENG_OFF = 4
 ENG_ON = 4
+ADDED = 640
 NDMA = 32
 
 
@@ -31,13 +32,13 @@ SCRATCH = {
     "KA": sb(128, F32), "KB": sb(128, F32),
     "NN": sb(256, F32), "DA": sb(768, F32), "DS": sb(768, F32), "ZA": sb(256, F32), "ZS": sb(512, F32),
     "OA": sb(64, U16), "OS": sb(128, U16), "KO": sb(768, U16), "II": sb(256, F32), "TT": sb(256, F32),
-    "AL": sb(A, F32), "F1": sb(A, F32), "Z": sb(A, F32), "Zb": sb(A, BF), "Xb": sb(512, BF), "Y": sb(A, F32),
+    "AL": sb(A, F32), "F1": sb(A, F32), "Z": sb(A, F32), "Zb": sb(A, BF), "Xb": sb(A, BF), "Y": sb(A, F32),
     "ML": ("sbuf", [128, 2, 8, 32], F32), "MS": sb(256, F32), "ones": sb(128, F32),
     "Lm": sb(512, F32), "Sm": sb(256, F32), "Sb": sb(256, BF), "Im": sb(128, F32), "Ib": sb(128, BF),
     "p0": sb(4, I32), "p1": sb(4, I32), "rm": sb(4, F32), "two": sb(64, I32), "pos": sb(64, F32),
     "J": ("psum", [128, 16, 2, 16], F32),
     "U0": ("psum", [128, 512], F32), "U1": ("psum", [128, 512], F32), "U2": ("psum", [128, 512], F32),
-    "R": ("psum", [128, 512], F32),
+    "U3": ("psum", [128, 512], F32), "U4": ("psum", [128, 512], F32), "R": ("psum", [128, 512], F32),
 }
 SEMAPHORES = ["cv", "cs", "ct", "cg"] + ["d%d" % i for i in range(NDMA)] + ["arr0", "arr1", "arr2", "out0", "out1", "out2"]
 
@@ -144,9 +145,10 @@ def rank_program(g, core, T, topo):
                                             remote_sem=T.sem["arr%d" % k], src=T[sbuf][:, i * width:(i + 1) * width],
                                             dst=T[land][:, base + me * width:base + (me + 1) * width]))
             return g.remote_dma_fused(tr, local_sem=T.sem["out%d" % k])
-        op(G, "r", send, [ap(sbuf)], [], sem="out%d" % k, val=n_out)
+        sent = op(G, "r", send, [ap(sbuf)], [], sem="out%d" % k, val=n_out)
         gather(S, c(land, base + me * width, base + (me + 1) * width), win, lst(me, 0, cols))
         op(None, "a", None, [], [c(land, base + r * width, base + (r + 1) * width) for r in others], sem="arr%d" % k, val=n_in)
+        return sent
 
     def steps(lv, buf, order):
         def lst(i):
@@ -177,11 +179,12 @@ def rank_program(g, core, T, topo):
     def widen(a, b):
         copy(S, c("W", a, b), c("Wb", a, b))
 
-    def load_level(lv, after, with_parts):
-        if with_parts:
-            load(SY, c("pt", lv * 512, lv * 512 + 512), T.parts[:, lv * 512:lv * 512 + 512], after)
+    def load_cap(lv, after):
         load(SY, c("capb", lv * A, lv * A + A), T.cap[:, lv * A:lv * A + A], after)
-        load(SY, c("stk", lv * A, lv * A + A), T.stock[:, lv * A:lv * A + A], after)
+
+    def load_stock(lv, after):
+        s0 = lv * A + (ADDED if lv == L - 1 else 0)
+        load(SY, c("stk", s0, lv * A + A), T.stock[:, s0:lv * A + A], after)
 
     load(S, ap("shp"), T.ship[:, :])
     load(SY, c("Wb", 0, M), T.sup[:, :])
@@ -211,13 +214,15 @@ def rank_program(g, core, T, topo):
         ts(c("pos", 8 * CUM[h], 8 * (CUM[h] + NCH[h])), c("two", 0, 8 * NCH[h]), c("rm", h, h + 1), Op.add)
     copy(V, ap("shu"), ap("shp"))
 
-    exchange(0, "sb0", SR, "Wb", M, c("Wb", 0, M), ("shu", 0))
+    sent = exchange(0, "sb0", SR, "Wb", M, c("Wb", 0, M), ("shu", 0))
     prepare(0)
     copy(V, ap("hnu"), ap("hnd"))
     copy(S, ap("Sb"), ap("Sm"))
     copy(S, ap("Ib"), ap("Im"))
     widen(0, 2048)
+    load_cap(0, [sent])
 
+    filled = []
     for lv in range(L):
         win = c("Wb" if lv == 0 else "W", 0, first(lv + 1))
         zn, sn = ("Zb", "Sb") if lv == 0 else ("Z", "Sm")
@@ -234,93 +239,117 @@ def rank_program(g, core, T, topo):
                 ko = c(kn, 16 * CUM[h], 16 * (CUM[h] + n))
                 keys.append(dma(SY, ko["ap"], T[src][15:128:16, x0:x0 + 256 * n], [c(src, x0, x0 + 256 * n)], [ko]))
         if lv == 0:
-            load_level(0, [keys[1]], False)
+            load_stock(0, [keys[1]])
             widen(2048, 3072)
         if lv < L - 1:
-            load_level(lv + 1, [keys[3]], True)
+            load(SY, c("pt", lv * 512 + 512, lv * 512 + 1024), T.parts[:, lv * 512 + 512:lv * 512 + 1024], [keys[3]])
+            load_cap(lv + 1, [keys[3]])
+            load_stock(lv + 1, [keys[3]])
+        if lv == L - 2:
+            filled.append(dma(G, T.y[:, 0:ADDED], T.stock[:, (L - 1) * A:(L - 1) * A + ADDED], [], [], [keys[3]]))
 
         def lists(h):
             n, m = NCH[h], CUM[h]
             n0, n1, k0, k1, d0 = 32 * m, 32 * (m + n), 16 * m, 16 * (m + n), lv * 256
             hi, n3, nn = c("NN", n0 + 2, n1, 4), c("NN", n0 + 3, n1, 4), c("NN", n0, n1)
-            calls = [
-                lambda: tt(c("NN", n0 + 1, n1, 2), c("KA", k0, k1), c("KB", k0, k1), Op.is_gt),
+            return [
                 lambda: tt(hi, c("KB", k0 + 1, k1, 2), c("KB", k0, k1, 2), Op.is_gt),
+                lambda: tt(c("NN", n0 + 1, n1, 2), c("KA", k0, k1), c("KB", k0, k1), Op.is_gt),
+                lambda: tt(c("ZS", 2 * n0 + 32 * n + 3, 2 * n1, 4), hi, c("pos", 8 * m, 8 * (m + n)), Op.add),
                 lambda: tt(n3, n3, hi, Op.max),
                 lambda: scan(c("ZA", n0, n1), nn, c("DA", d0 + n0, d0 + n1)),
-                lambda: copy(V, c("OA", 8 * m, 8 * (m + n)), c("ZA", n0 + 3, n1, 4)),
-                lambda: tt(c("ZS", 2 * n0 + 32 * n + 3, 2 * n1, 4), hi, c("pos", 8 * m, 8 * (m + n)), Op.add),
                 lambda: scan(c("ZS", 2 * n0, 2 * n0 + 32 * n), nn, c("DS", d0 + n0, d0 + n1)),
+                lambda: copy(V, c("OA", 8 * m, 8 * (m + n)), c("ZA", n0 + 3, n1, 4)),
                 lambda: copy(V, c("OS", k0, k1), c("ZS", 2 * n0 + 3, 2 * n1, 4))]
-            for k in ((0, 1, 2, 3, 4, 5, 6, 7), (1, 0, 5, 2, 3, 6, 4, 7))[h]:
-                calls[k]()
 
-        def alt(a, b):
-            gather(S, c("AL", a, b), win, c("OA", a // 16, b // 16))
+        def alt(q, a, b):
+            gather(q, c("AL", a, b), win, c("OA", a // 16, b // 16))
 
-        def sib(h, a, b):
-            o = 8 * CUM[h] + a // 16
+        cut = (0, 128, 384, 640, 896, A)
+
+        def sib(k):
+            a, b = cut[k], cut[k + 1]
+            o = 8 * CUM[k >= 2] + a // 16
             gmin(c("F1", a, b), win, c("OS", o, o + (b - a) // 16), c("AL", a, b))
 
-        def pair(h, un, u0, a, b):
-            n, m = NCH[h], CUM[h]
+        def pair(k):
+            a, b = cut[k], cut[k + 1]
+            n, m = NCH[k >= 2], CUM[k >= 2]
             o = 8 * (m + n) + a // 16
             gmin(c(zn, a, b), c("PP", 256 * m, 256 * (m + n)), c("OS", o, o + (b - a) // 16), c("F1", a, b))
             for x, y in ((a, min(b, A // 2)), (max(a, A // 2), b)):
                 if x < y:
                     s0 = 128 * (x >= A // 2)
-                    mm(c(un, x - u0, y - u0), c(sn, s0, s0 + 128), c(zn, x, y), True, True)
+                    mm(c("U%d" % k, x - a, y - a), c(sn, s0, s0 + 128), c(zn, x, y), True, True)
 
-        def capped(un, a, b):
-            u = c(un, 0, b - a)
-            tt(u, u, c("capb", lv * A + a, lv * A + b), Op.min)
+        def capped(k):
+            a, b = cut[k], cut[k + 1]
+            u = c("U%d" % k, 0, b - a)
+            out = u if k > 2 or lv == 1 else c("Xb" if lv == 0 else "Y", a, b)
+            tt(out, u, c("capb", lv * A + a, lv * A + b), Op.min)
 
-        def stocked(un, a, b):
-            tt(c(dst, db + a, db + b), c(un, 0, b - a), c("stk", lv * A + a, lv * A + b), Op.add)
-            if lv == L - 1:
-                dma(SY, T.y[:, a:b], T.Y[:, a:b], [c("Y", a, b)], [])
+        def stocked(k):
+            a, b = cut[k], cut[k + 1]
+            if k > 2 or lv == 1:
+                tt(c(dst, db + a, db + b), c("U%d" % k, 0, b - a), c("stk", lv * A + a, lv * A + b), Op.add)
+                return
+            if k == 0:
+                return
+            a = 0 if k == 1 else a
+            if lv == 0:
+                r = c("R", 0, b - a)
+                mm(r, ap("Ib"), c("Xb", a, b), True, False)
+                mm(r, ap("Ib"), c("stk", a, b), False, True)
+                copy(S, c(dst, db + a, db + b), r)
+            else:
+                op(G, "d", lambda: g.dma_start(T.y[:, a:b], T.Y[:, a:b], accum_op=Op.add), [c("Y", a, b)], [], filled)
 
-        a1, a2, a3 = 128, 128 * NCH[0], 768
-        lists(0)
-        alt(0, a1)
-        alt(a1, a2)
-        sib(0, 0, a1)
-        pair(0, "U0", 0, 0, a1)
-        sib(0, a1, a2)
-        pair(0, "U0", 0, a1, a2)
+        ca, cb = lists(0), lists(1)
+        for call in ca:
+            call()
+        alt(V, 0, cut[1])
+        alt(S, cut[1], cut[2])
+        sib(0)
+        sib(1)
+        pair(0)
+        pair(1)
         if lv == 0:
             widen(3072, 4096)
-        lists(1)
-        alt(a2, a3)
-        alt(a3, A)
-        if lv == 0:
-            tt(c("Xb", 0, a2), c("U0", 0, a2), c("capb", 0, a2), Op.min)
-            mm(c("R", 0, a2), ap("Ib"), c("Xb", 0, a2), True, False)
-            mm(c("R", 0, a2), ap("Ib"), c("stk", 0, a2), False, True)
-            copy(S, c(dst, db, db + a2), c("R", 0, a2))
-            sib(1, a2, a3)
-            sib(1, a3, A)
-            pair(1, "U1", a2, a2, a3)
+        for call in cb[:4]:
+            call()
+        capped(0)
+        for call in cb[4:]:
+            call()
+        for k in (2, 3, 4):
+            alt(S, cut[k], cut[k + 1])
+        stocked(0)
+        capped(1)
+        if lv != 1:
+            stocked(1)
+        sib(2)
+        if lv == 1:
+            stocked(1)
+            pair(2)
+            sib(3)
         else:
-            capped("U0", 0, a2)
-            sib(1, a2, a3)
-            stocked("U0", 0, a2)
-            pair(1, "U1", a2, a2, a3)
-            sib(1, a3, A)
-        pair(1, "U2", a3, a3, A)
-        capped("U1", a2, a3)
-        if lv == 0:
-            capped("U2", a3, A)
-            stocked("U1", a2, a3)
-        else:
-            stocked("U1", a2, a3)
-            capped("U2", a3, A)
-        stocked("U2", a3, A)
+            sib(3)
+            pair(2)
+        sib(4)
+        pair(3)
+        capped(2)
+        pair(4)
+        stocked(2)
+        capped(3)
+        capped(4)
+        stocked(3)
+        stocked(4)
         if lv < L - 1:
             exchange(lv + 1, "sb%d" % (lv + 1), SA, "W", db + A, c("W", db, db + A), ("hnu", lv * 32))
             prepare(lv + 1)
             if lv == 0:
                 widen(M, first(1))
+        else:
+            dma(SY, T.y[:, ADDED:A], T.Y[:, ADDED:A], [c("Y", ADDED, A)], [])
 
     csem = {V: "cv", S: "cs", PE: "ct", G: "cg"}
     count = {k: 0 for k in csem}

@@ -6,11 +6,14 @@ M, A, L, SR, SA, NR = 4096, 1024, 3, 320, 128, 4
 F32, BF, I32, U16 = "float32", "bfloat16", "int32", "uint16"
 NCH = (3, 5)
 CUM = (0, NCH[0])
-PIECE = 256
+PIECES = ((128, 320, 320), (320, 320, 320, 320))
 ENG_OFF = 4
 ENG_ON = 4
 ADDED = 640
 NDMA = 32
+HEAD = "a0 a1 a2 a3 a4 a5 a6 a7 v0 t1 s0 s1 %s b0 b1 p0 b3 b2 p1 b4 b5 b6 c0 b7 t2 t3 t4 "
+TAIL = "c1 k1 s2 s3 p2 s4 p3 p4 c2 k2 c3 c4 k3 k4"
+ORDER = (HEAD % "w0" + TAIL, HEAD % "" + "k0 c1 s2 k1 p2 s3 s4 p3 c2 p4 k2 c3 c4 k3 k4", HEAD % "" + TAIL)
 
 
 def first(l):
@@ -40,7 +43,7 @@ SCRATCH = {
     "U0": ("psum", [128, 512], F32), "U1": ("psum", [128, 512], F32), "U2": ("psum", [128, 512], F32),
     "U3": ("psum", [128, 512], F32), "U4": ("psum", [128, 512], F32), "R": ("psum", [128, 512], F32),
 }
-SEMAPHORES = ["cv", "cs", "ct", "cg"] + ["d%d" % i for i in range(NDMA)] + ["arr0", "arr1", "arr2", "out0", "out1", "out2"]
+SEMAPHORES = ["cv", "cs", "ct", "cg"] + ["d%d" % i for i in range(NDMA)] + ["arr0", "arr1", "arr2", "out0", "out1", "out2", "out3"]
 
 
 def masks_for(core, dsts, topo):
@@ -123,10 +126,9 @@ def rank_program(g, core, T, topo):
     others = [(me + k) % NR for k in range(1, NR)]
     others.sort(key=lambda r: topo.chip(cores[r]) == topo.chip(core))
     mk = masks_for(core, [cores[r] for r in others], topo)
-    n_out = sum(v[1] for v in mk.values())
     n_in = sum(masks_for(cores[r], [cores[x] for x in range(NR) if x != r], topo)[core][1] for r in others)
 
-    def exchange(k, sbuf, width, land, base, win, offs):
+    def exchange(k, sbuf, width, land, base, win, offs, calls):
         cols = width // 16
         h = cols // 2 - (cols // 2) % 2
 
@@ -137,15 +139,17 @@ def rank_program(g, core, T, topo):
         gather(V, c(sbuf, 2 * width, 2 * width + 16 * h), win, lst(others[2], 0, h))
         gather(S, c(sbuf, 2 * width + 16 * h, 3 * width), win, lst(others[2], h, cols))
 
-        def send():
+        def send(which, sem):
             tr = []
-            for i, r in enumerate(others):
+            for i in which:
+                r = others[i]
                 rid, pid = topo.addr(cores[r])[:2]
                 tr.append(RemoteDMATransfer(dst_ids=[DstId(rid=rid, pnc=pid)], dma_engine_mask=mk[cores[r]][0],
                                             remote_sem=T.sem["arr%d" % k], src=T[sbuf][:, i * width:(i + 1) * width],
                                             dst=T[land][:, base + me * width:base + (me + 1) * width]))
-            return g.remote_dma_fused(tr, local_sem=T.sem["out%d" % k])
-        sent = op(G, "r", send, [ap(sbuf)], [], sem="out%d" % k, val=n_out)
+            return g.remote_dma_fused(tr, local_sem=T.sem[sem])
+        sent = [op(G, "r", lambda which=which, sem=sem: send(which, sem), [c(sbuf, i * width, (i + 1) * width) for i in which], [],
+                   sem=sem, val=sum(mk[cores[others[i]]][1] for i in which)) for which, sem in calls]
         gather(S, c(land, base + me * width, base + (me + 1) * width), win, lst(me, 0, cols))
         op(None, "a", None, [], [c(land, base + r * width, base + (r + 1) * width) for r in others], sem="arr%d" % k, val=n_in)
         return sent
@@ -187,9 +191,8 @@ def rank_program(g, core, T, topo):
         load(SY, c("stk", s0, lv * A + A), T.stock[:, s0:lv * A + A], after)
 
     load(S, ap("shp"), T.ship[:, :])
-    load(SY, c("Wb", 0, M), T.sup[:, :])
-    load(SY, c("pt", 0, 512), T.parts[:, 0:512])
-    load(SY, ap("hnd"), T.hand[:, :])
+    raw = load(SY, c("Wb", 0, M), T.sup[:, :])
+    load(SY, c("pt", 0, 512), T.parts[:, 0:512], [raw])
     p0, two = ap("p0"), ap("two")
     op(G, "c", lambda: g.iota(p0["ap"], [[1, 4]], 0, 1), [], [p0])
     op(G, "c", lambda: g.iota(two["ap"], [[2, 64]], 0, 0), [], [two])
@@ -214,13 +217,12 @@ def rank_program(g, core, T, topo):
         ts(c("pos", 8 * CUM[h], 8 * (CUM[h] + NCH[h])), c("two", 0, 8 * NCH[h]), c("rm", h, h + 1), Op.add)
     copy(V, ap("shu"), ap("shp"))
 
-    sent = exchange(0, "sb0", SR, "Wb", M, c("Wb", 0, M), ("shu", 0))
+    sent = exchange(0, "sb0", SR, "Wb", M, c("Wb", 0, M), ("shu", 0), [((0, 1), "out0"), ((2,), "out3")])
     prepare(0)
-    copy(V, ap("hnu"), ap("hnd"))
     copy(S, ap("Sb"), ap("Sm"))
     copy(S, ap("Ib"), ap("Im"))
     widen(0, 2048)
-    load_cap(0, [sent])
+    load_cap(0, sent)
 
     filled = []
     for lv in range(L):
@@ -229,12 +231,13 @@ def rank_program(g, core, T, topo):
         dst, db = ("W", first(lv + 1)) if lv < L - 1 else ("Y", 0)
         keys = []
         for h in range(2):
-            n, x0 = NCH[h], 256 * CUM[h]
-            for a in range(0, 256 * n, PIECE):
+            n, x0, a = NCH[h], 256 * CUM[h], 0
+            for w in PIECES[h]:
                 k0 = lv * 256 + 32 * CUM[h] + a // 16
-                vv = c("VV", x0 + a, x0 + a + PIECE)
-                gather(S, vv, win, c("KO", k0, k0 + PIECE // 16))
-                gmin(c("PP", x0 + a, x0 + a + PIECE), win, c("KO", k0 + 16 * n, k0 + 16 * n + PIECE // 16), vv)
+                vv = c("VV", x0 + a, x0 + a + w)
+                gather(V if x0 + a == 0 else S, vv, win, c("KO", k0, k0 + w // 16))
+                gmin(c("PP", x0 + a, x0 + a + w), win, c("KO", k0 + 16 * n, k0 + 16 * n + w // 16), vv)
+                a += w
             for kn, src in (("KA", "VV"), ("KB", "PP")):
                 ko = c(kn, 16 * CUM[h], 16 * (CUM[h] + n))
                 keys.append(dma(SY, ko["ap"], T[src][15:128:16, x0:x0 + 256 * n], [c(src, x0, x0 + 256 * n)], [ko]))
@@ -243,6 +246,8 @@ def rank_program(g, core, T, topo):
             widen(2048, 3072)
         if lv < L - 1:
             load(SY, c("pt", lv * 512 + 512, lv * 512 + 1024), T.parts[:, lv * 512 + 512:lv * 512 + 1024], [keys[3]])
+            if lv == 0:
+                load(SY, ap("hnd"), T.hand[:, :])
             load_cap(lv + 1, [keys[3]])
             load_stock(lv + 1, [keys[3]])
         if lv == L - 2:
@@ -262,10 +267,11 @@ def rank_program(g, core, T, topo):
                 lambda: copy(V, c("OA", 8 * m, 8 * (m + n)), c("ZA", n0 + 3, n1, 4)),
                 lambda: copy(V, c("OS", k0, k1), c("ZS", 2 * n0 + 3, 2 * n1, 4))]
 
-        def alt(q, a, b):
-            gather(q, c("AL", a, b), win, c("OA", a // 16, b // 16))
-
         cut = (0, 128, 384, 640, 896, A)
+
+        def alt(q, k):
+            a, b = cut[k], cut[k + 1]
+            gather(q, c("AL", a, b), win, c("OA", a // 16, b // 16))
 
         def sib(k):
             a, b = cut[k], cut[k + 1]
@@ -293,8 +299,6 @@ def rank_program(g, core, T, topo):
             if k > 2 or lv == 1:
                 tt(c(dst, db + a, db + b), c("U%d" % k, 0, b - a), c("stk", lv * A + a, lv * A + b), Op.add)
                 return
-            if k == 0:
-                return
             a = 0 if k == 1 else a
             if lv == 0:
                 r = c("R", 0, b - a)
@@ -305,46 +309,14 @@ def rank_program(g, core, T, topo):
                 op(G, "d", lambda: g.dma_start(T.y[:, a:b], T.Y[:, a:b], accum_op=Op.add), [c("Y", a, b)], [], filled)
 
         ca, cb = lists(0), lists(1)
-        for call in ca:
-            call()
-        alt(V, 0, cut[1])
-        alt(S, cut[1], cut[2])
-        sib(0)
-        sib(1)
-        pair(0)
-        pair(1)
-        if lv == 0:
-            widen(3072, 4096)
-        for call in cb[:4]:
-            call()
-        capped(0)
-        for call in cb[4:]:
-            call()
-        for k in (2, 3, 4):
-            alt(S, cut[k], cut[k + 1])
-        stocked(0)
-        capped(1)
-        if lv != 1:
-            stocked(1)
-        sib(2)
-        if lv == 1:
-            stocked(1)
-            pair(2)
-            sib(3)
-        else:
-            sib(3)
-            pair(2)
-        sib(4)
-        pair(3)
-        capped(2)
-        pair(4)
-        stocked(2)
-        capped(3)
-        capped(4)
-        stocked(3)
-        stocked(4)
+        calls = {"a": lambda k: ca[k](), "b": lambda k: cb[k](), "v": lambda k: alt(V, k), "t": lambda k: alt(S, k),
+                 "s": sib, "p": pair, "c": capped, "k": stocked, "w": lambda k: widen(3072, 4096)}
+        for w in ORDER[lv].split():
+            if lv == 0 and w == "c3":
+                copy(V, ap("hnu"), ap("hnd"))
+            calls[w[0]](int(w[1:]))
         if lv < L - 1:
-            exchange(lv + 1, "sb%d" % (lv + 1), SA, "W", db + A, c("W", db, db + A), ("hnu", lv * 32))
+            exchange(lv + 1, "sb%d" % (lv + 1), SA, "W", db + A, c("W", db, db + A), ("hnu", lv * 32), [((0, 1, 2), "out%d" % (lv + 1))])
             prepare(lv + 1)
             if lv == 0:
                 widen(M, first(1))

import numpy as np
from concourse.bass import DstId, RemoteDMATransfer
from concourse.mybir import AluOpType, ActivationFunctionType

M, A, L, SR, SA, NR = 4096, 1024, 3, 320, 128, 4
F32, BF, I32, U16 = "float32", "bfloat16", "int32", "uint16"
NCH = (3, 5)
CUM = (0, NCH[0])
PIECES = ((128, 320, 320), (320, 320, 320, 320))
ENG_OFF = 4
ENG_ON = 4
ADDED = 640
NDMA = 32
HEAD = "a0 a1 a2 a3 a4 a5 a6 a7 v0 t1 s0 s1 %s b0 b1 p0 b3 b2 p1 b4 b5 b6 c0 b7 t2 t3 t4 "
TAIL = "c1 k1 s2 s3 p2 s4 p3 p4 c2 k2 c3 c4 k3 k4"
ORDER = (HEAD % "w0" + TAIL, HEAD % "" + "k0 c1 s2 k1 p2 s3 s4 p3 c2 p4 k2 c3 c4 k3 k4", HEAD % "" + TAIL)


def first(l):
    return M + NR * SR + (l - 1) * (A + NR * SA)


def sb(n, d):
    return ("sbuf", [128, n], d)


SCRATCH = {
    "Wb": sb(first(1), BF),
    "W": sb(first(3), F32),
    "capb": sb(L * A, BF), "stk": sb(L * A, BF), "pt": sb(1536, I32),
    "shp": sb(80, I32), "shu": sb(80, U16), "hnd": sb(64, I32), "hnu": sb(64, U16),
    "sb0": sb(3 * SR, BF), "sb1": sb(3 * SA, F32), "sb2": sb(3 * SA, F32),
    "VV": sb(2048, F32),
    "PP": sb(2048, F32),
    "KA": sb(128, F32), "KB": sb(128, F32),
    "NN": sb(256, F32), "DA": sb(768, F32), "DS": sb(768, F32), "ZA": sb(256, F32), "ZS": sb(512, F32),
    "OA": sb(64, U16), "OS": sb(128, U16), "KO": sb(768, U16), "II": sb(256, F32), "TT": sb(256, F32),
    "AL": sb(A, F32), "F1": sb(A, F32), "Z": sb(A, F32), "Zb": sb(A, BF), "Xb": sb(A, BF), "Y": sb(A, F32),
    "ML": ("sbuf", [128, 2, 8, 32], F32), "MS": sb(256, F32), "ones": sb(128, F32),
    "Lm": sb(512, F32), "Sm": sb(256, F32), "Sb": sb(256, BF), "Im": sb(128, F32), "Ib": sb(128, BF),
    "p0": sb(4, I32), "p1": sb(4, I32), "rm": sb(4, F32), "two": sb(64, I32), "pos": sb(64, F32),
    "J": ("psum", [128, 16, 2, 16], F32),
    "U0": ("psum", [128, 512], F32), "U1": ("psum", [128, 512], F32), "U2": ("psum", [128, 512], F32),
    "U3": ("psum", [128, 512], F32), "U4": ("psum", [128, 512], F32), "R": ("psum", [128, 512], F32),
}
SEMAPHORES = ["cv", "cs", "ct", "cg"] + ["d%d" % i for i in range(NDMA)] + ["arr0", "arr1", "arr2", "out0", "out1", "out2", "out3"]


def masks_for(core, dsts, topo):
    far = [d for d in dsts if topo.chip(d) != topo.chip(core)]
    near = [d for d in dsts if topo.chip(d) == topo.chip(core)]
    used, out = set(), {}
    for part, n in ((far, ENG_OFF), (near, ENG_ON)):
        seen = set()
        for i, d in enumerate(part):
            al = [e for e in topo.engines(core, d) if e not in used]
            per = len(al) // len(part)
            mine = al[i * per:(i + 1) * per]
            out[d] = mine[::max(1, len(mine) // n)][:n]
            seen |= set(al)
        used |= seen
    return {d: (sum(1 << e for e in v), len(v)) for d, v in out.items()}


def rank_program(g, core, T, topo):
    me = T.rank_of(core)
    if me is None:
        return
    cores = list(T.cores)
    Q = {"v": g.vector, "s": g.scalar, "t": g.tensor, "g": g, "y": g.sync}
    ops = []
    V, S, PE, G, SY = "v", "s", "t", "g", "y"
    Op = AluOpType
    grid = {n: np.arange(int(np.prod(s[1][1:]))).reshape(s[1][1:]) for n, s in SCRATCH.items()}

    def ap(name, *idx):
        idx = idx or (slice(None),)
        return {"ap": T[name][(slice(None),) + tuple(idx)], "buf": name, "cols": grid[name][tuple(idx)].ravel()}

    def c(name, a, b, step=None):
        return ap(name, slice(a, b, step))

    def op(q, kind, fn, reads, writes, after=(), sem=None, val=None):
        ops.append({"q": q, "kind": kind, "fn": fn, "r": reads, "w": writes, "after": list(after), "sem": sem, "val": val})
        return len(ops) - 1

    def ind(win, off):
        return win["ap"].indirect(off["ap"])

    def copy(q, out, in_):
        if q == V:
            return op(V, "c", lambda: g.vector.tensor_copy(out["ap"], in_["ap"]), [in_], [out])
        return op(S, "c", lambda: g.scalar.activation(out["ap"], in_["ap"], ActivationFunctionType.Copy), [in_], [out])

    def gather(q, out, win, off):
        if q == V:
            return op(V, "c", lambda: g.vector.tensor_copy(out["ap"], ind(win, off)), [win, off], [out])
        return op(S, "c", lambda: g.scalar.activation(out["ap"], ind(win, off), ActivationFunctionType.Copy), [win, off], [out])

    def gmin(out, win, off, in1):
        return op(V, "c", lambda: g.vector.tensor_tensor(out["ap"], ind(win, off), in1["ap"], Op.min), [win, off, in1], [out])

    def tt(out, in0, in1, alu):
        return op(V, "c", lambda: g.vector.tensor_tensor(out["ap"], in0["ap"], in1["ap"], alu), [in0, in1], [out])

    def ts(out, in0, scalar, alu):
        col = [scalar] if isinstance(scalar, dict) else []
        sc = scalar["ap"] if col else scalar
        return op(V, "c", lambda: g.vector.tensor_scalar(out["ap"], in0["ap"], sc, None, alu), [in0] + col, [out])

    def scan(out, d0, d1):
        return op(V, "c", lambda: g.vector.tensor_tensor_scan(out["ap"], d0["ap"], d1["ap"], 0.0, Op.mult, Op.add), [d0, d1], [out])

    def memset(out, v):
        return op(V, "c", lambda: g.vector.memset(out["ap"], v), [], [out])

    def mm(out, lhsT, rhs, start, stop):
        return op(PE, "c", lambda: g.tensor.matmul(out["ap"], lhsT["ap"], rhs["ap"], start, stop), [lhsT, rhs], [out])

    def dma(q, out_ap, in_ap, reads, writes, after=()):
        return op(q, "d", lambda: Q[q].dma_start(out_ap, in_ap), reads, writes, after)

    def load(q, out, src, after=()):
        return dma(q, out["ap"], src, [], [out], after)

    others = [(me + k) % NR for k in range(1, NR)]
    others.sort(key=lambda r: topo.chip(cores[r]) == topo.chip(core))
    mk = masks_for(core, [cores[r] for r in others], topo)
    n_in = sum(masks_for(cores[r], [cores[x] for x in range(NR) if x != r], topo)[core][1] for r in others)

    def exchange(k, sbuf, width, land, base, win, offs, calls):
        cols = width // 16
        h = cols // 2 - (cols // 2) % 2

        def lst(r, a, b):
            return c(offs[0], offs[1] + r * cols + a, offs[1] + r * cols + b)
        gather(V, c(sbuf, 0, width), win, lst(others[0], 0, cols))
        gather(S, c(sbuf, width, 2 * width), win, lst(others[1], 0, cols))
        gather(V, c(sbuf, 2 * width, 2 * width + 16 * h), win, lst(others[2], 0, h))
        gather(S, c(sbuf, 2 * width + 16 * h, 3 * width), win, lst(others[2], h, cols))

        def send(which, sem):
            tr = []
            for i in which:
                r = others[i]
                rid, pid = topo.addr(cores[r])[:2]
                tr.append(RemoteDMATransfer(dst_ids=[DstId(rid=rid, pnc=pid)], dma_engine_mask=mk[cores[r]][0],
                                            remote_sem=T.sem["arr%d" % k], src=T[sbuf][:, i * width:(i + 1) * width],
                                            dst=T[land][:, base + me * width:base + (me + 1) * width]))
            return g.remote_dma_fused(tr, local_sem=T.sem[sem])
        sent = [op(G, "r", lambda which=which, sem=sem: send(which, sem), [c(sbuf, i * width, (i + 1) * width) for i in which], [],
                   sem=sem, val=sum(mk[cores[others[i]]][1] for i in which)) for which, sem in calls]
        gather(S, c(land, base + me * width, base + (me + 1) * width), win, lst(me, 0, cols))
        op(None, "a", None, [], [c(land, base + r * width, base + (r + 1) * width) for r in others], sem="arr%d" % k, val=n_in)
        return sent

    def steps(lv, buf, order):
        def lst(i):
            return c("pt", lv * 512 + order[i] * 64, lv * 512 + order[i] * 64 + 64)
        for k in range(3):
            tt(c(buf, lv * 256 + k, lv * 256 + 256, 4), lst(3 - k), lst(2 - k), Op.subtract)
        copy(V, c(buf, lv * 256 + 3, lv * 256 + 256, 4), lst(0))

    def prepare(lv):
        pc = lv * 512
        for e in range(2):
            for b in range(2):
                comp = (2, 0)[b] + e
                copy(V, c("II", e * 128 + b, e * 128 + 128, 2), c("pt", pc + comp * 64, pc + comp * 64 + 64))
        for u in range(2):
            for e in range(2):
                mm(ap("J", slice(0, 8), u), c("Lm", (2 * e + u) * 128, (2 * e + u + 1) * 128), c("II", e * 128, e * 128 + 128), e == 0, e == 1)
        steps(lv, "DA", (4, 5, 6, 7))
        steps(lv, "DS", (1, 0, 3, 2))
        j, t = ap("J", slice(0, 8)), ap("TT")
        op(V, "c", lambda: g.vector.transpose(t["ap"], j["ap"]), [j], [t])
        for h in range(2):
            k0 = lv * 256 + 32 * CUM[h]
            for ch in range(NCH[h]):
                bb = CUM[h] + ch
                copy(V, c("KO", k0 + ch, k0 + 32 * NCH[h], NCH[h]), c("TT", bb * 32, bb * 32 + 32))

    def widen(a, b):
        copy(S, c("W", a, b), c("Wb", a, b))

    def load_cap(lv, after):
        load(SY, c("capb", lv * A, lv * A + A), T.cap[:, lv * A:lv * A + A], after)

    def load_stock(lv, after):
        s0 = lv * A + (ADDED if lv == L - 1 else 0)
        load(SY, c("stk", s0, lv * A + A), T.stock[:, s0:lv * A + A], after)

    load(S, ap("shp"), T.ship[:, :])
    raw = load(SY, c("Wb", 0, M), T.sup[:, :])
    load(SY, c("pt", 0, 512), T.parts[:, 0:512], [raw])
    p0, two = ap("p0"), ap("two")
    op(G, "c", lambda: g.iota(p0["ap"], [[1, 4]], 0, 1), [], [p0])
    op(G, "c", lambda: g.iota(two["ap"], [[2, 64]], 0, 0), [], [two])
    for e in range(2):
        memset(ap("ML", e, slice(None), slice(16 * e, 16 * e + 16)), 1.0)
        memset(ap("ML", e, slice(None), slice(16 - 16 * e, 32 - 16 * e)), 0.0)
    memset(ap("MS"), 1.0)
    memset(ap("ones"), 1.0)
    memset(c("NN", 0, 256, 4), 0.0)
    memset(c("MS", 0, 256, 16), 0.0)
    memset(c("MS", 129, 256, 16), 0.0)

    def select(out, in_, pattern, base):
        op(G, "c", lambda: g.affine_select(out["ap"], in_["ap"], pattern, Op.is_equal, 0.0, base, 1), [in_], [out])
    select(ap("Lm"), ap("ML"), [[16, 2], [-16, 2], [-1, 128]], 0)
    select(ap("Sm"), ap("MS"), [[1, 2], [-1, 128]], 1)
    select(ap("Im"), ap("ones"), [[-1, 128]], 0)
    ts(ap("p1"), p0, 15, Op.bitwise_and)
    for h in range(2):
        ts(c("rm", h, h + 1), c("p1", 0, 1), float(16 * NCH[h]), Op.mult)
    for h in range(2):
        ts(c("pos", 8 * CUM[h], 8 * (CUM[h] + NCH[h])), c("two", 0, 8 * NCH[h]), c("rm", h, h + 1), Op.add)
    copy(V, ap("shu"), ap("shp"))

    sent = exchange(0, "sb0", SR, "Wb", M, c("Wb", 0, M), ("shu", 0), [((0, 1), "out0"), ((2,), "out3")])
    prepare(0)
    copy(S, ap("Sb"), ap("Sm"))
    copy(S, ap("Ib"), ap("Im"))
    widen(0, 2048)
    load_cap(0, sent)

    filled = []
    for lv in range(L):
        win = c("Wb" if lv == 0 else "W", 0, first(lv + 1))
        zn, sn = ("Zb", "Sb") if lv == 0 else ("Z", "Sm")
        dst, db = ("W", first(lv + 1)) if lv < L - 1 else ("Y", 0)
        keys = []
        for h in range(2):
            n, x0, a = NCH[h], 256 * CUM[h], 0
            for w in PIECES[h]:
                k0 = lv * 256 + 32 * CUM[h] + a // 16
                vv = c("VV", x0 + a, x0 + a + w)
                gather(V if x0 + a == 0 else S, vv, win, c("KO", k0, k0 + w // 16))
                gmin(c("PP", x0 + a, x0 + a + w), win, c("KO", k0 + 16 * n, k0 + 16 * n + w // 16), vv)
                a += w
            for kn, src in (("KA", "VV"), ("KB", "PP")):
                ko = c(kn, 16 * CUM[h], 16 * (CUM[h] + n))
                keys.append(dma(SY, ko["ap"], T[src][15:128:16, x0:x0 + 256 * n], [c(src, x0, x0 + 256 * n)], [ko]))
        if lv == 0:
            load_stock(0, [keys[1]])
            widen(2048, 3072)
        if lv < L - 1:
            load(SY, c("pt", lv * 512 + 512, lv * 512 + 1024), T.parts[:, lv * 512 + 512:lv * 512 + 1024], [keys[3]])
            if lv == 0:
                load(SY, ap("hnd"), T.hand[:, :])
            load_cap(lv + 1, [keys[3]])
            load_stock(lv + 1, [keys[3]])
        if lv == L - 2:
            filled.append(dma(G, T.y[:, 0:ADDED], T.stock[:, (L - 1) * A:(L - 1) * A + ADDED], [], [], [keys[3]]))

        def lists(h):
            n, m = NCH[h], CUM[h]
            n0, n1, k0, k1, d0 = 32 * m, 32 * (m + n), 16 * m, 16 * (m + n), lv * 256
            hi, n3, nn = c("NN", n0 + 2, n1, 4), c("NN", n0 + 3, n1, 4), c("NN", n0, n1)
            return [
                lambda: tt(hi, c("KB", k0 + 1, k1, 2), c("KB", k0, k1, 2), Op.is_gt),
                lambda: tt(c("NN", n0 + 1, n1, 2), c("KA", k0, k1), c("KB", k0, k1), Op.is_gt),
                lambda: tt(c("ZS", 2 * n0 + 32 * n + 3, 2 * n1, 4), hi, c("pos", 8 * m, 8 * (m + n)), Op.add),
                lambda: tt(n3, n3, hi, Op.max),
                lambda: scan(c("ZA", n0, n1), nn, c("DA", d0 + n0, d0 + n1)),
                lambda: scan(c("ZS", 2 * n0, 2 * n0 + 32 * n), nn, c("DS", d0 + n0, d0 + n1)),
                lambda: copy(V, c("OA", 8 * m, 8 * (m + n)), c("ZA", n0 + 3, n1, 4)),
                lambda: copy(V, c("OS", k0, k1), c("ZS", 2 * n0 + 3, 2 * n1, 4))]

        cut = (0, 128, 384, 640, 896, A)

        def alt(q, k):
            a, b = cut[k], cut[k + 1]
            gather(q, c("AL", a, b), win, c("OA", a // 16, b // 16))

        def sib(k):
            a, b = cut[k], cut[k + 1]
            o = 8 * CUM[k >= 2] + a // 16
            gmin(c("F1", a, b), win, c("OS", o, o + (b - a) // 16), c("AL", a, b))

        def pair(k):
            a, b = cut[k], cut[k + 1]
            n, m = NCH[k >= 2], CUM[k >= 2]
            o = 8 * (m + n) + a // 16
            gmin(c(zn, a, b), c("PP", 256 * m, 256 * (m + n)), c("OS", o, o + (b - a) // 16), c("F1", a, b))
            for x, y in ((a, min(b, A // 2)), (max(a, A // 2), b)):
                if x < y:
                    s0 = 128 * (x >= A // 2)
                    mm(c("U%d" % k, x - a, y - a), c(sn, s0, s0 + 128), c(zn, x, y), True, True)

        def capped(k):
            a, b = cut[k], cut[k + 1]
            u = c("U%d" % k, 0, b - a)
            out = u if k > 2 or lv == 1 else c("Xb" if lv == 0 else "Y", a, b)
            tt(out, u, c("capb", lv * A + a, lv * A + b), Op.min)

        def stocked(k):
            a, b = cut[k], cut[k + 1]
            if k > 2 or lv == 1:
                tt(c(dst, db + a, db + b), c("U%d" % k, 0, b - a), c("stk", lv * A + a, lv * A + b), Op.add)
                return
            a = 0 if k == 1 else a
            if lv == 0:
                r = c("R", 0, b - a)
                mm(r, ap("Ib"), c("Xb", a, b), True, False)
                mm(r, ap("Ib"), c("stk", a, b), False, True)
                copy(S, c(dst, db + a, db + b), r)
            else:
                op(G, "d", lambda: g.dma_start(T.y[:, a:b], T.Y[:, a:b], accum_op=Op.add), [c("Y", a, b)], [], filled)

        ca, cb = lists(0), lists(1)
        calls = {"a": lambda k: ca[k](), "b": lambda k: cb[k](), "v": lambda k: alt(V, k), "t": lambda k: alt(S, k),
                 "s": sib, "p": pair, "c": capped, "k": stocked, "w": lambda k: widen(3072, 4096)}
        for w in ORDER[lv].split():
            if lv == 0 and w == "c3":
                copy(V, ap("hnu"), ap("hnd"))
            calls[w[0]](int(w[1:]))
        if lv < L - 1:
            exchange(lv + 1, "sb%d" % (lv + 1), SA, "W", db + A, c("W", db, db + A), ("hnu", lv * 32), [((0, 1, 2), "out%d" % (lv + 1))])
            prepare(lv + 1)
            if lv == 0:
                widen(M, first(1))
        else:
            dma(SY, T.y[:, ADDED:A], T.Y[:, ADDED:A], [c("Y", ADDED, A)], [])

    csem = {V: "cv", S: "cs", PE: "ct", G: "cg"}
    count = {k: 0 for k in csem}
    known = {q: {} for q in Q}
    hist = {n: [] for n in SCRATCH}
    final = {}
    nd = 0
    for i, o in enumerate(ops):
        deps = set(o["after"])
        acc = [(a, False) for a in o["r"]] + [(a, True) for a in o["w"]]
        for a, wr in acc:
            psum = SCRATCH[a["buf"]][0] == "psum"
            mask = np.zeros(grid[a["buf"]].size, bool)
            mask[a["cols"]] = True
            for j, m2, w2 in hist[a["buf"]]:
                if j == i:
                    continue
                same = ops[j]["q"] == o["q"]
                if psum and not same:
                    deps.add(j)
                elif psum and o["q"] == PE:
                    continue
                elif (wr or w2) and (mask & m2).any():
                    deps.add(j)
            hist[a["buf"]].append((i, mask, wr))
        q = o["q"]
        if o["kind"] == "a":
            o["ev"], o["clock"] = (o["sem"], o["val"]), {o["sem"]: o["val"]}
            final[o["sem"]] = o["val"]
            continue
        need = {}
        for j in deps:
            s, v = ops[j]["ev"]
            if v > need.get(s, (0, None))[0]:
                need[s] = (v, j)
        for s, (v, j) in sorted(need.items(), key=lambda kv: -kv[1][1]):
            if known[q].get(s, 0) >= v:
                continue
            Q[q].wait_ge(T.sem[s], v)
            for s2, v2 in ops[j]["clock"].items():
                known[q][s2] = max(known[q].get(s2, 0), v2)
        ins = o["fn"]()
        if o["kind"] == "c":
            count[q] += 1
            ev = (csem[q], count[q])
            ins.then_inc(T.sem[ev[0]], 1)
        elif o["kind"] == "d":
            ev = ("d%d" % nd, 16)
            nd += 1
            ins.then_inc(T.sem[ev[0]], 16)
        else:
            ev = (o["sem"], o["val"])
        o["ev"] = ev
        o["clock"] = dict(known[q])
        o["clock"][ev[0]] = ev[1]
        final[ev[0]] = ev[1]
    for s, v in final.items():
        if max(known[q].get(s, 0) for q in Q) < v:
            g.sync.wait_ge(T.sem[s], v)
